import numpy as np
import ml_dtypes


def mxq(x, axis, fmt="e4m3"):
    dtype, down = {"e4m3": (ml_dtypes.float8_e4m3fn, 7), "e5m2": (ml_dtypes.float8_e5m2, 14)}[fmt]
    v = np.moveaxis(np.asarray(x, np.float32).astype(ml_dtypes.bfloat16).astype(np.float64), axis, -1)
    blocks = v.reshape(v.shape[:-1] + (-1, 32))
    amax = np.abs(blocks).max(-1, keepdims=True)
    byte = np.maximum(np.where(amax > 0, np.frexp(amax)[1] - 1 + 127, 0) - down, 1)
    scale = np.exp2(byte - 127.0)
    codes = (blocks / scale).astype(np.float32).astype(dtype).astype(np.float64)
    return np.moveaxis((codes * scale).reshape(v.shape), -1, axis)


WIDE = False


def mx_kscale(k):
    if not WIDE:
        return np.ones(k)
    levels = np.array([10, -10, 5, -5, 0])
    if k % 512:
        return np.exp2(np.random.permutation(np.resize(levels, k // 32))).repeat(32)
    a = np.empty((k // 512, 16))
    for p in range(k // 512):
        a[p, :8] = np.random.permutation(np.resize(levels, 8))
        for g in range(8):
            far = levels[np.abs(levels - a[p, g]) >= 10]
            a[p, g + 8] = far[np.random.randint(len(far))]
    return np.exp2(a.ravel()).repeat(32)


def f64(x):
    return np.asarray(x).astype(np.float64)


def striped(idx):
    return np.tile(idx.reshape(-1, 16).T, (8, 1)).astype(np.uint16)


def unstriped(offs):
    return offs[:16].T.reshape(-1).astype(np.int64)


def striped8(idx):
    return np.concatenate([x.reshape(-1, 16).T for x in idx]).astype(np.uint16)


def runs(offs, k):
    lists = np.stack([offs[16 * r : 16 * r + 16].T.reshape(-1) for r in range(8)]).astype(np.int64)
    return lists[np.arange(k) % 512 // 64]


def pack_weight(w):
    k, n = w.shape
    w = f64(np.asarray(w, np.float32).astype(ml_dtypes.bfloat16)).reshape(k // 32, 32, n)
    amax = np.abs(w).max(1)
    byte = np.clip(np.where(amax > 0, np.frexp(amax)[1] - 1 + 127 - 7, 1), 1, 254)
    scaled = (w * np.exp2(127.0 - byte)[:, None, :]).reshape(k, n).astype(np.float32)
    words = np.ascontiguousarray(scaled.reshape(k // 512, 128, 4, n).transpose(0, 1, 3, 2)).astype(ml_dtypes.float8_e4m3fn).view(np.uint8)
    return words, np.ascontiguousarray(byte.astype(np.uint8).reshape(k // 512, 16, n))


def unpack_weight(words, scales):
    g, p, n, _ = words.shape
    vals = np.ascontiguousarray(words).view(ml_dtypes.float8_e4m3fn).astype(np.float64) * np.repeat(np.exp2(scales.astype(np.float64) - 127.0), 8, axis=1)[..., None]
    return vals.transpose(0, 1, 3, 2).reshape(g * 512, n)


K, T, S, G, H = 512, 1024, 512, 2048, 512


def setup_inputs():
    n = np.random.standard_normal
    s = mx_kscale(K)[:, None]
    packed_xT = pack_weight(n((K, T)) * s)
    packed_dT = pack_weight(n((K, G)) / s)
    return {
        "x_words": packed_xT[0],
        "x_scales": packed_xT[1],
        "d_words": packed_dT[0],
        "d_scales": packed_dT[1],
        "gs": (np.random.uniform(0.5, 1.5, (K, 1)) * s).astype(np.float32),
        "offs": striped(np.random.permutation(T)[:S]),
        "k1": striped8(np.random.randint(0, G, (8, H))),
        "n1": striped8(np.stack([np.random.permutation(S) for _ in range(8)])),
        "n2": striped8(np.stack([np.random.permutation(S) for _ in range(8)])),
        "n3": striped8(np.stack([np.random.permutation(S) for _ in range(8)])),
        "k2": striped8(np.random.randint(0, G, (8, H))),
        "n4": striped8(np.stack([np.random.permutation(S) for _ in range(8)])),
        "n5": striped8(np.stack([np.random.permutation(S) for _ in range(8)])),
    }


def reference(x_words, x_scales, d_words, d_scales, gs, offs, k1, n1, n2, n3, k2, n4, n5):
    d_k2 = unpack_weight(d_words, d_scales)[np.arange(K)[:, None], runs(k2, K)]
    d_k1 = unpack_weight(d_words, d_scales)[np.arange(K)[:, None], runs(k1, K)]
    xq = unpack_weight(x_words, x_scales)[:, unstriped(offs)]
    h = 0.0625 * (d_k1.T @ xq)
    b1 = h[np.arange(H)[:, None], runs(n1, H)]
    b2 = h[np.arange(H)[:, None], runs(n2, H)]
    b3 = h[np.arange(H)[:, None], runs(n3, H)]
    z = f64(gs) * (np.maximum(np.maximum(b1, b2), b3) - (0.5 * (np.maximum(np.minimum(b1, b2), np.minimum(np.maximum(b1, b2), b3)))))
    h2 = 0.0625 * ((d_k2.T @ mxq(z, 0, "e4m3")))
    return 0.75 * (h2[np.arange(H)[:, None], runs(n4, H)] + h2[np.arange(H)[:, None], runs(n5, H)]) - h2

@@ -1,0 +1,169 @@
+from contextlib import ExitStack
+
+import concourse.mybir as mybir
+
+K, T, S, G, H = 512, 1024, 512, 2048, 512
+FLOPS = 2 * 2 * K * H * S
+
+F32 = mybir.dt.float32
+BF16 = mybir.dt.bfloat16
+I32 = mybir.dt.int32
+U32 = mybir.dt.uint32
+U16 = mybir.dt.uint16
+U8 = mybir.dt.uint8
+FP8X4 = mybir.dt.float8_e4m3fn_x4
+ALU = mybir.AluOpType
+ACT = mybir.ActivationFunctionType
+
+P = 128
+PACK = 4
+BLK = 256
+NBLK = S // BLK
+LCOL = BLK // 16
+
+
+def tile_picked_codetop2lap_none_p_kernel(tc, x_words, x_scales, d_words, d_scales, gs, offs, k1, n1, n2, n3, k2, n4, n5, out):
+    nc = tc.nc
+    with ExitStack() as ctx:
+        keep = ctx.enter_context(tc.tile_pool(name="keep", bufs=1))
+        psum = ctx.enter_context(tc.psum_pool(name="psum", bufs=1))
+
+        def sb(shape, dtype, name, tag=None):
+            return keep.tile(shape, dtype, name=name, tag=tag or name, align_bytes=64)
+
+        def load_list(src, name):
+            lst = sb([P, S // 16], U16, name)
+            nc.sync.dma_start(lst[:], src)
+            return lst
+
+        d_bytes = sb([P, G], U8, "d_bytes")
+        x_bytes = sb([P, T], U8, "x_bytes")
+        nc.vector.memset(d_bytes[:].bitcast(I32), 0)
+        nc.gpsimd.memset(x_bytes[:].bitcast(I32), 0)
+
+        offs_l = load_list(offs, "offs_l")
+        x_tab = sb([P, T], I32, "x_tab")
+        nc.sync.dma_start(x_tab[:], x_words[0].rearrange("p n t -> p (n t)").bitcast(I32))
+        k1_l = load_list(k1, "k1_l")
+        d_rows = d_scales[0].bitcast(I32)
+        for e in range(2):
+            nc.sync.dma_start(d_bytes[:].bitcast(I32)[e:P:16, :], d_rows[e:16:2, :])
+        d_tab = sb([P, G], I32, "d_tab")
+        nc.sync.dma_start(d_tab[:], d_words[0].rearrange("p n t -> p (n t)").bitcast(I32))
+        x_rows = x_scales[0].bitcast(I32)
+        for r in range(4):
+            nc.sync.dma_start(x_bytes[:].bitcast(I32)[r:P:32, :], x_rows[r:16:4, :])
+        k2_l = load_list(k2, "k2_l")
+        n1_l = load_list(n1, "n1_l")
+        n2_l = load_list(n2, "n2_l")
+        n3_l = load_list(n3, "n3_l")
+        gain = sb([P, PACK], F32, "gain")
+        nc.sync.dma_start(gain[:], gs.rearrange("(p t) o -> p (t o)", t=PACK))
+        n4_l = load_list(n4, "n4_l")
+        n5_l = load_list(n5, "n5_l")
+        half_gain = sb([P, PACK], F32, "half_gain")
+        nc.scalar.activation(half_gain[:], gain[:], ACT.Copy, scale=0.5)
+
+        def deal(dst, src):
+            nc.vector.tensor_copy(dst[:].rearrange("p (t m) -> p m t", t=PACK), src[:].rearrange("p (m t) -> p m t", t=PACK))
+
+        def code_scales(lst, name):
+            picked = sb([P, H], U8, name + "_picked")
+            nc.vector.tensor_copy(picked[:], d_bytes[:].indirect(lst[:]))
+            plane = sb([P, H], U8, name + "_plane")
+            deal(plane, picked)
+            rows = plane[:].bitcast(I32)
+            for e in range(2):
+                nc.scalar.dma_start(rows[2 + e:P:32, :], rows[16 + e:P:32, :])
+            return plane
+
+        def code_words(lst, name, tag=None):
+            picked = sb([P, H], U32, name + "_picked", tag)
+            nc.vector.tensor_copy(picked[:], d_tab[:].bitcast(U32).indirect(lst[:]))
+            words = sb([P, H], U32, name + "_dealt")
+            deal(words, picked)
+            return words
+
+        x_sel = sb([P, S], U32, "x_sel")
+        nc.vector.tensor_copy(x_sel[:], x_tab[:].bitcast(U32).indirect(offs_l[:]))
+        w1_plane = code_scales(k1_l, "w1s")
+        w1_words = code_words(k1_l, "w1w")
+        x_plane = sb([P, S], U8, "x_plane")
+        nc.vector.tensor_copy(x_plane[:], x_bytes[:].indirect(offs_l[:]))
+
+        h = []
+        for t in range(PACK):
+            cols = slice(t * P, (t + 1) * P)
+            acc = psum.tile([P, S], F32, name="acc1", tag="bank%d" % t)
+            nc.tensor.matmul_mx(out=acc[:], lhsT=w1_words[:, cols].bitcast(FP8X4), lhsT_scale=w1_plane[:, cols],
+                                rhs=x_sel[:].bitcast(FP8X4), rhs_scale=x_plane[:], start=True, stop=True)
+            ht = sb([P, S], F32, "h%d" % t)
+            nc.scalar.activation(ht[:], acc[:], ACT.Copy, scale=0.0625)
+            h.append(ht)
+
+        w2_plane = code_scales(k2_l, "w2s")
+
+        z_words, z_plane = [], []
+        w2_words = None
+        for b in range(NBLK):
+            lc = slice(b * LCOL, (b + 1) * LCOL)
+
+            def pair(name, tag=None):
+                return [sb([P, 2, BLK], F32, "%s%d_%d" % (name, b, u), tag and "%s_%d" % (tag, u)) for u in range(2)]
+
+            a = pair("a", "hold" if b == 1 else None)
+            u_ = pair("u")
+            mx = pair("mx")
+            au = pair("au")
+            gm = pair("gm")
+            for t in range(PACK):
+                nc.vector.tensor_copy(a[t // 2][:, t % 2, :], h[t][:].indirect(n1_l[:, lc]))
+            for t in range(PACK):
+                nc.vector.tensor_tensor(u_[t // 2][:, t % 2, :], h[t][:].indirect(n2_l[:, lc]), a[t // 2][:, t % 2, :], ALU.subtract)
+            for u in range(2):
+                nc.vector.scalar_tensor_tensor(mx[u][:], u_[u][:], 0.0, a[u][:], ALU.max, ALU.add)
+                nc.scalar.activation(au[u][:], u_[u][:], ACT.Abs, scale=0.5)
+            v = pair("v", "hold" if b == 0 else None)
+            for t in range(PACK):
+                nc.vector.tensor_tensor(v[t // 2][:, t % 2, :], h[t][:].indirect(n3_l[:, lc]), mx[t // 2][:, t % 2, :], ALU.subtract)
+                nc.scalar.activation(gm[t // 2][:, t % 2, :], mx[t // 2][:, t % 2, :], ACT.Copy, scale=half_gain[:, t:t + 1])
+            low = pair("low")
+            y = pair("y", "late" if b == NBLK - 1 else None)
+            for u in range(2):
+                nc.vector.scalar_tensor_tensor(low[u][:], v[u][:], -0.5, au[u][:], ALU.mult, ALU.min)
+            for u in range(2):
+                nc.vector.tensor_tensor(y[u][:], v[u][:], low[u][:], ALU.max)
+            z = sb([P, PACK, BLK], F32, "z%d" % b)
+            for t in range(PACK):
+                nc.vector.scalar_tensor_tensor(z[:, t, :], y[t // 2][:, t % 2, :], gain[:, t:t + 1], gm[t // 2][:, t % 2, :], ALU.mult, ALU.add)
+            zb = sb([P, BLK, PACK], BF16, "zb%d" % b)
+            nc.scalar.copy(zb[:].rearrange("p (c i) t -> p c t i", i=4), z[:].rearrange("p t (c i) -> p c t i", i=4))
+            if b == NBLK - 1:
+                w2_words = code_words(k2_l, "w2w", "late_0")
+            zw = sb([P, BLK], U32, "zw%d" % b)
+            zp = sb([P, BLK], U8, "zp%d" % b)
+            nc.vector.quantize_mx(out=zw[:].bitcast(FP8X4), scales=zp[:], in_=zb[:].rearrange("p j t -> p (j t)"))
+            z_words.append(zw)
+            z_plane.append(zp)
+
+        out_t = out.rearrange("(p t) j -> t p j", t=PACK)
+        for t in range(PACK):
+            cols = slice(t * P, (t + 1) * P)
+            win = sb([P, S], F32, "win%d" % t)
+            neg = sb([P, S], F32, "neg%d" % t)
+            for b in range(NBLK):
+                js = slice(b * BLK, (b + 1) * BLK)
+                acc = psum.tile([P, BLK], F32, name="acc2", tag="bank%d" % ((2 * t + b + 4) % 8))
+                nc.tensor.matmul_mx(out=acc[:], lhsT=w2_words[:, cols].bitcast(FP8X4), lhsT_scale=w2_plane[:, cols],
+                                    rhs=z_words[b][:].bitcast(FP8X4), rhs_scale=z_plane[b][:], start=True, stop=True)
+                nc.scalar.activation(win[:, js], acc[:], ACT.Copy, scale=0.75 * 0.0625)
+                nc.scalar.activation(neg[:, js], acc[:], ACT.Copy, scale=-0.0625)
+            part = sb([P, S], F32, "part%d" % t)
+            res = [sb([P, BLK], F32, "res%d_%d" % (t, b)) for b in range(NBLK)]
+            for b in range(NBLK):
+                js = slice(b * BLK, (b + 1) * BLK)
+                nc.vector.tensor_tensor(part[:, js], win[:].indirect(n4_l[:, b * LCOL:(b + 1) * LCOL]), neg[:, js], ALU.add)
+            for b in range(NBLK):
+                js = slice(b * BLK, (b + 1) * BLK)
+                nc.vector.tensor_tensor(res[b][:], win[:].indirect(n5_l[:, b * LCOL:(b + 1) * LCOL]), part[:, js], ALU.add)
+                nc.sync.dma_start(out_t[t][:, js], res[b][:])

@@ -40,6 +40,11 @@ def tile_picked_codetop2lap_none_p_kernel(tc, x_words, x_scales, d_words, d_scal
         x_bytes = sb([P, T], U8, "x_bytes")
         nc.vector.memset(d_bytes[:].bitcast(I32), 0)
         nc.gpsimd.memset(x_bytes[:].bitcast(I32), 0)
+        rowwin = [sb([P, S], F32, "rowwin%d" % t) for t in range(PACK)]
+        halves = [slice(b * BLK, (b + 1) * BLK) for b in range(NBLK)]
+
+        def entries(lst, js):
+            return lst[:, js.start // 16:js.stop // 16]
 
         offs_l = load_list(offs, "offs_l")
         x_tab = sb([P, T], I32, "x_tab")
@@ -48,11 +53,11 @@ def tile_picked_codetop2lap_none_p_kernel(tc, x_words, x_scales, d_words, d_scal
         d_rows = d_scales[0].bitcast(I32)
         for e in range(2):
             nc.sync.dma_start(d_bytes[:].bitcast(I32)[e:P:16, :], d_rows[e:16:2, :])
-        d_tab = sb([P, G], I32, "d_tab")
-        nc.sync.dma_start(d_tab[:], d_words[0].rearrange("p n t -> p (n t)").bitcast(I32))
         x_rows = x_scales[0].bitcast(I32)
         for r in range(4):
             nc.sync.dma_start(x_bytes[:].bitcast(I32)[r:P:32, :], x_rows[r:16:4, :])
+        d_tab = sb([P, G], I32, "d_tab")
+        nc.sync.dma_start(d_tab[:], d_words[0].rearrange("p n t -> p (n t)").bitcast(I32))
         k2_l = load_list(k2, "k2_l")
         n1_l = load_list(n1, "n1_l")
         n2_l = load_list(n2, "n2_l")
@@ -62,16 +67,20 @@ def tile_picked_codetop2lap_none_p_kernel(tc, x_words, x_scales, d_words, d_scal
         n4_l = load_list(n4, "n4_l")
         n5_l = load_list(n5, "n5_l")
         half_gain = sb([P, PACK], F32, "half_gain")
-        nc.scalar.activation(half_gain[:], gain[:], ACT.Copy, scale=0.5)
+        nc.gpsimd.tensor_scalar_mul(half_gain[:], gain[:], 0.5)
 
-        def deal(dst, src):
-            nc.vector.tensor_copy(dst[:].rearrange("p (t m) -> p m t", t=PACK), src[:].rearrange("p (m t) -> p m t", t=PACK))
+        def deal(dst, src, line):
+            nc.vector.tensor_copy(dst[:].rearrange("p (t c i) -> p c t i", t=PACK, i=line),
+                                  src[:].rearrange("p (c i t) -> p c t i", t=PACK, i=line))
 
-        def code_scales(lst, name):
-            picked = sb([P, H], U8, name + "_picked")
+        def pick_scales(lst, name, tag=None):
+            picked = sb([P, H], U8, name, tag)
             nc.vector.tensor_copy(picked[:], d_bytes[:].indirect(lst[:]))
+            return picked
+
+        def code_plane(picked, name):
             plane = sb([P, H], U8, name + "_plane")
-            deal(plane, picked)
+            deal(plane, picked, 16)
             rows = plane[:].bitcast(I32)
             for e in range(2):
                 nc.scalar.dma_start(rows[2 + e:P:32, :], rows[16 + e:P:32, :])
@@ -81,89 +90,96 @@ def tile_picked_codetop2lap_none_p_kernel(tc, x_words, x_scales, d_words, d_scal
             picked = sb([P, H], U32, name + "_picked", tag)
             nc.vector.tensor_copy(picked[:], d_tab[:].bitcast(U32).indirect(lst[:]))
             words = sb([P, H], U32, name + "_dealt")
-            deal(words, picked)
+            deal(words, picked, 4)
             return words
 
         x_sel = sb([P, S], U32, "x_sel")
         nc.vector.tensor_copy(x_sel[:], x_tab[:].bitcast(U32).indirect(offs_l[:]))
-        w1_plane = code_scales(k1_l, "w1s")
-        w1_words = code_words(k1_l, "w1w")
+        w1_bytes = pick_scales(k1_l, "w1_bytes")
         x_plane = sb([P, S], U8, "x_plane")
         nc.vector.tensor_copy(x_plane[:], x_bytes[:].indirect(offs_l[:]))
+        w1_plane = code_plane(w1_bytes, "w1s")
+        w1_words = code_words(k1_l, "w1w")
 
-        h = []
         for t in range(PACK):
             cols = slice(t * P, (t + 1) * P)
             acc = psum.tile([P, S], F32, name="acc1", tag="bank%d" % t)
             nc.tensor.matmul_mx(out=acc[:], lhsT=w1_words[:, cols].bitcast(FP8X4), lhsT_scale=w1_plane[:, cols],
                                 rhs=x_sel[:].bitcast(FP8X4), rhs_scale=x_plane[:], start=True, stop=True)
-            ht = sb([P, S], F32, "h%d" % t)
-            nc.scalar.activation(ht[:], acc[:], ACT.Copy, scale=0.0625)
-            h.append(ht)
+            nc.scalar.activation(rowwin[t][:], acc[:], ACT.Copy, scale=0.0625)
 
-        w2_plane = code_scales(k2_l, "w2s")
+        w2_plane = code_plane(pick_scales(k2_l, "w2_bytes", "w1w_picked"), "w2s")
 
-        z_words, z_plane = [], []
+        def pair(name, width, tag=None):
+            return [sb([P, 2, width], F32, "%s_%d" % (name, q), tag and "%s_%d" % (tag, q)) for q in range(2)]
+
+        a, du, mx, au, gm = (pair(name, S) for name in ("a", "du", "mx", "au", "gm"))
+        for t in range(PACK):
+            for js in halves:
+                nc.vector.tensor_copy(a[t // 2][:, t % 2, js], rowwin[t][:].indirect(entries(n1_l, js)))
+            for js in halves:
+                nc.vector.tensor_tensor(du[t // 2][:, t % 2, js], rowwin[t][:].indirect(entries(n2_l, js)), a[t // 2][:, t % 2, js], ALU.subtract)
+        for q in range(2):
+            nc.vector.scalar_tensor_tensor(mx[q][:], du[q][:], 0.0, a[q][:], ALU.max, ALU.add)
+            nc.scalar.activation(au[q][:], du[q][:], ACT.Abs, scale=0.5)
+        for t in range(PACK):
+            nc.scalar.activation(gm[t // 2][:, t % 2, :], mx[t // 2][:, t % 2, :], ACT.Copy, scale=half_gain[:, t:t + 1])
+
+        z_words = sb([P, S], U32, "z_words")
+        z_plane = sb([P, S], U8, "z_plane")
         w2_words = None
         for b in range(NBLK):
-            lc = slice(b * LCOL, (b + 1) * LCOL)
-
-            def pair(name, tag=None):
-                return [sb([P, 2, BLK], F32, "%s%d_%d" % (name, b, u), tag and "%s_%d" % (tag, u)) for u in range(2)]
-
-            a = pair("a", "hold" if b == 1 else None)
-            u_ = pair("u")
-            mx = pair("mx")
-            au = pair("au")
-            gm = pair("gm")
+            js = slice(b * BLK, (b + 1) * BLK)
+            v = pair("v%d" % b, BLK, "v")
             for t in range(PACK):
-                nc.vector.tensor_copy(a[t // 2][:, t % 2, :], h[t][:].indirect(n1_l[:, lc]))
-            for t in range(PACK):
-                nc.vector.tensor_tensor(u_[t // 2][:, t % 2, :], h[t][:].indirect(n2_l[:, lc]), a[t // 2][:, t % 2, :], ALU.subtract)
-            for u in range(2):
-                nc.vector.scalar_tensor_tensor(mx[u][:], u_[u][:], 0.0, a[u][:], ALU.max, ALU.add)
-                nc.scalar.activation(au[u][:], u_[u][:], ACT.Abs, scale=0.5)
-            v = pair("v", "hold" if b == 0 else None)
-            for t in range(PACK):
-                nc.vector.tensor_tensor(v[t // 2][:, t % 2, :], h[t][:].indirect(n3_l[:, lc]), mx[t // 2][:, t % 2, :], ALU.subtract)
-                nc.scalar.activation(gm[t // 2][:, t % 2, :], mx[t // 2][:, t % 2, :], ACT.Copy, scale=half_gain[:, t:t + 1])
-            low = pair("low")
-            y = pair("y", "late" if b == NBLK - 1 else None)
-            for u in range(2):
-                nc.vector.scalar_tensor_tensor(low[u][:], v[u][:], -0.5, au[u][:], ALU.mult, ALU.min)
-            for u in range(2):
-                nc.vector.tensor_tensor(y[u][:], v[u][:], low[u][:], ALU.max)
+                nc.vector.tensor_tensor(v[t // 2][:, t % 2, :], rowwin[t][:].indirect(n3_l[:, b * LCOL:(b + 1) * LCOL]),
+                                        mx[t // 2][:, t % 2, js], ALU.subtract)
+            low = pair("low%d" % b, BLK)
+            y = pair("y%d" % b, BLK, "late" if b == NBLK - 1 else None)
+            for q in range(2):
+                nc.vector.scalar_tensor_tensor(low[q][:], v[q][:], -0.5, au[q][:, :, js], ALU.mult, ALU.min)
+            for q in range(2):
+                nc.vector.tensor_tensor(y[q][:], v[q][:], low[q][:], ALU.max)
             z = sb([P, PACK, BLK], F32, "z%d" % b)
             for t in range(PACK):
-                nc.vector.scalar_tensor_tensor(z[:, t, :], y[t // 2][:, t % 2, :], gain[:, t:t + 1], gm[t // 2][:, t % 2, :], ALU.mult, ALU.add)
+                nc.vector.scalar_tensor_tensor(z[:, t, :], y[t // 2][:, t % 2, :], gain[:, t:t + 1], gm[t // 2][:, t % 2, js], ALU.mult, ALU.add)
             zb = sb([P, BLK, PACK], BF16, "zb%d" % b)
             nc.scalar.copy(zb[:].rearrange("p (c i) t -> p c t i", i=4), z[:].rearrange("p t (c i) -> p c t i", i=4))
             if b == NBLK - 1:
                 w2_words = code_words(k2_l, "w2w", "late_0")
-            zw = sb([P, BLK], U32, "zw%d" % b)
-            zp = sb([P, BLK], U8, "zp%d" % b)
-            nc.vector.quantize_mx(out=zw[:].bitcast(FP8X4), scales=zp[:], in_=zb[:].rearrange("p j t -> p (j t)"))
-            z_words.append(zw)
-            z_plane.append(zp)
+            nc.vector.quantize_mx(out=z_words[:, js].bitcast(FP8X4), scales=z_plane[:, js], in_=zb[:].rearrange("p j t -> p (j t)"))
 
         out_t = out.rearrange("(p t) j -> t p j", t=PACK)
-        for t in range(PACK):
+        neg = [sb([P, S], F32, "neg%d" % t) for t in range(PACK)]
+        part = [sb([P, S], F32, "part%d" % t) for t in range(PACK)]
+        res = [sb([P, S], F32, "res%d" % t) for t in range(PACK)]
+
+        def product2(t, js, bank):
             cols = slice(t * P, (t + 1) * P)
-            win = sb([P, S], F32, "win%d" % t)
-            neg = sb([P, S], F32, "neg%d" % t)
-            for b in range(NBLK):
-                js = slice(b * BLK, (b + 1) * BLK)
-                acc = psum.tile([P, BLK], F32, name="acc2", tag="bank%d" % ((2 * t + b + 4) % 8))
-                nc.tensor.matmul_mx(out=acc[:], lhsT=w2_words[:, cols].bitcast(FP8X4), lhsT_scale=w2_plane[:, cols],
-                                    rhs=z_words[b][:].bitcast(FP8X4), rhs_scale=z_plane[b][:], start=True, stop=True)
-                nc.scalar.activation(win[:, js], acc[:], ACT.Copy, scale=0.75 * 0.0625)
-                nc.scalar.activation(neg[:, js], acc[:], ACT.Copy, scale=-0.0625)
-            part = sb([P, S], F32, "part%d" % t)
-            res = [sb([P, BLK], F32, "res%d_%d" % (t, b)) for b in range(NBLK)]
-            for b in range(NBLK):
-                js = slice(b * BLK, (b + 1) * BLK)
-                nc.vector.tensor_tensor(part[:, js], win[:].indirect(n4_l[:, b * LCOL:(b + 1) * LCOL]), neg[:, js], ALU.add)
-            for b in range(NBLK):
-                js = slice(b * BLK, (b + 1) * BLK)
-                nc.vector.tensor_tensor(res[b][:], win[:].indirect(n5_l[:, b * LCOL:(b + 1) * LCOL]), part[:, js], ALU.add)
-                nc.sync.dma_start(out_t[t][:, js], res[b][:])
+            acc = psum.tile([P, js.stop - js.start], F32, name="acc2", tag="bank%d" % bank)
+            nc.tensor.matmul_mx(out=acc[:], lhsT=w2_words[:, cols].bitcast(FP8X4), lhsT_scale=w2_plane[:, cols],
+                                rhs=z_words[:, js].bitcast(FP8X4), rhs_scale=z_plane[:, js], start=True, stop=True)
+            return acc
+
+        def first(t, js):
+            nc.vector.tensor_tensor(part[t][:, js], rowwin[t][:].indirect(n4_l[:, js.start // 16:js.stop // 16]), neg[t][:, js], ALU.add)
+
+        def second(t, js):
+            nc.vector.tensor_tensor(res[t][:, js], rowwin[t][:].indirect(n5_l[:, js.start // 16:js.stop // 16]), part[t][:, js], ALU.add)
+            nc.sync.dma_start(out_t[t][:, js], res[t][:, js])
+
+        whole = slice(0, S)
+        acc0 = [product2(0, js, 4 + b) for b, js in enumerate(halves)]
+        for b, js in enumerate(halves):
+            nc.scalar.activation(rowwin[0][:, js], acc0[b][:], ACT.Copy, scale=0.75 * 0.0625)
+        nc.vector.tensor_scalar_mul(neg[0][:, halves[0]], acc0[0][:], -0.0625)
+        nc.scalar.activation(neg[0][:, halves[1]], acc0[1][:], ACT.Copy, scale=-0.0625)
+        for t in range(1, PACK):
+            acc = product2(t, whole, t)
+            nc.scalar.activation(rowwin[t][:, whole], acc[:], ACT.Copy, scale=0.75 * 0.0625)
+            nc.scalar.activation(neg[t][:], acc[:], ACT.Copy, scale=-0.0625)
+        for t in range(PACK):
+            for js in halves:
+                first(t, js)
+            for js in halves:
+                second(t, js)

@@ -1,6 +1,7 @@
 from contextlib import ExitStack
 
 import concourse.mybir as mybir
+from concourse.masks import make_identity
 
 K, T, S, G, H = 512, 1024, 512, 2048, 512
 FLOPS = 2 * 2 * K * H * S
@@ -69,36 +70,35 @@ def tile_picked_codetop2lap_none_p_kernel(tc, x_words, x_scales, d_words, d_scal
         half_gain = sb([P, PACK], F32, "half_gain")
         nc.gpsimd.tensor_scalar_mul(half_gain[:], gain[:], 0.5)
 
-        def deal(dst, src, line):
-            nc.vector.tensor_copy(dst[:].rearrange("p (t c i) -> p c t i", t=PACK, i=line),
-                                  src[:].rearrange("p (c i t) -> p c t i", t=PACK, i=line))
-
-        def pick_scales(lst, name, tag=None):
-            picked = sb([P, H], U8, name, tag)
-            nc.vector.tensor_copy(picked[:], d_bytes[:].indirect(lst[:]))
+        def pick(window, lst, dtype, name, tag=None):
+            picked = sb([P, H], dtype, name, tag)
+            for js in halves:
+                nc.vector.tensor_copy(picked[:, js], window.indirect(entries(lst, js)))
             return picked
 
-        def code_plane(picked, name):
-            plane = sb([P, H], U8, name + "_plane")
-            deal(plane, picked, 16)
+        def deal(picked, dtype, line, name):
+            dealt = sb([P, H], dtype, name)
+            for js in halves:
+                ms = slice(js.start // PACK, js.stop // PACK)
+                nc.vector.tensor_copy(dealt[:].rearrange("p (t m) -> p t m", t=PACK)[:, :, ms].rearrange("p t (c i) -> p c t i", i=line),
+                                      picked[:, js].rearrange("p (c i t) -> p c t i", t=PACK, i=line))
+            return dealt
+
+        def code_plane(lst, name, tag=None):
+            plane = deal(pick(d_bytes[:], lst, U8, name + "_picked", tag), U8, 16, name + "_plane")
             rows = plane[:].bitcast(I32)
             for e in range(2):
                 nc.scalar.dma_start(rows[2 + e:P:32, :], rows[16 + e:P:32, :])
             return plane
 
         def code_words(lst, name, tag=None):
-            picked = sb([P, H], U32, name + "_picked", tag)
-            nc.vector.tensor_copy(picked[:], d_tab[:].bitcast(U32).indirect(lst[:]))
-            words = sb([P, H], U32, name + "_dealt")
-            deal(words, picked, 4)
-            return words
+            return deal(pick(d_tab[:].bitcast(U32), lst, U32, name + "_picked", tag), U32, 4, name + "_dealt")
 
         x_sel = sb([P, S], U32, "x_sel")
         nc.vector.tensor_copy(x_sel[:], x_tab[:].bitcast(U32).indirect(offs_l[:]))
-        w1_bytes = pick_scales(k1_l, "w1_bytes")
+        w1_plane = code_plane(k1_l, "w1s")
         x_plane = sb([P, S], U8, "x_plane")
         nc.vector.tensor_copy(x_plane[:], x_bytes[:].indirect(offs_l[:]))
-        w1_plane = code_plane(w1_bytes, "w1s")
         w1_words = code_words(k1_l, "w1w")
 
         for t in range(PACK):
@@ -108,7 +108,7 @@ def tile_picked_codetop2lap_none_p_kernel(tc, x_words, x_scales, d_words, d_scal
                                 rhs=x_sel[:].bitcast(FP8X4), rhs_scale=x_plane[:], start=True, stop=True)
             nc.scalar.activation(rowwin[t][:], acc[:], ACT.Copy, scale=0.0625)
 
-        w2_plane = code_plane(pick_scales(k2_l, "w2_bytes", "w1w_picked"), "w2s")
+        w2_plane = code_plane(k2_l, "w2s", "w1w_picked")
 
         def pair(name, width, tag=None):
             return [sb([P, 2, width], F32, "%s_%d" % (name, q), tag and "%s_%d" % (tag, q)) for q in range(2)]
@@ -125,6 +125,8 @@ def tile_picked_codetop2lap_none_p_kernel(tc, x_words, x_scales, d_words, d_scal
         for t in range(PACK):
             nc.scalar.activation(gm[t // 2][:, t % 2, :], mx[t // 2][:, t % 2, :], ACT.Copy, scale=half_gain[:, t:t + 1])
 
+        ident = sb([P, P], F32, "ident")
+        make_identity(nc, ident[:])
         z_words = sb([P, S], U32, "z_words")
         z_plane = sb([P, S], U8, "z_plane")
         w2_words = None
@@ -135,19 +137,36 @@ def tile_picked_codetop2lap_none_p_kernel(tc, x_words, x_scales, d_words, d_scal
                 nc.vector.tensor_tensor(v[t // 2][:, t % 2, :], rowwin[t][:].indirect(n3_l[:, b * LCOL:(b + 1) * LCOL]),
                                         mx[t // 2][:, t % 2, js], ALU.subtract)
             low = pair("low%d" % b, BLK)
-            y = pair("y%d" % b, BLK, "late" if b == NBLK - 1 else None)
+            y = pair("y%d" % b, BLK)
             for q in range(2):
                 nc.vector.scalar_tensor_tensor(low[q][:], v[q][:], -0.5, au[q][:, :, js], ALU.mult, ALU.min)
             for q in range(2):
                 nc.vector.tensor_tensor(y[q][:], v[q][:], low[q][:], ALU.max)
-            z = sb([P, PACK, BLK], F32, "z%d" % b)
-            for t in range(PACK):
-                nc.vector.scalar_tensor_tensor(z[:, t, :], y[t // 2][:, t % 2, :], gain[:, t:t + 1], gm[t // 2][:, t % 2, js], ALU.mult, ALU.add)
-            zb = sb([P, BLK, PACK], BF16, "zb%d" % b)
-            nc.scalar.copy(zb[:].rearrange("p (c i) t -> p c t i", i=4), z[:].rearrange("p t (c i) -> p c t i", i=4))
-            if b == NBLK - 1:
+            if b == 0:
+                gy = pair("gy", BLK)
+                for t in range(PACK):
+                    nc.scalar.activation(gy[t // 2][:, t % 2, :], y[t // 2][:, t % 2, :], ACT.Copy, scale=gain[:, t:t + 1])
+                back = psum.tile([P, BLK // P, 2, P], F32, name="back", tag="bank0")
+                for c in range(BLK // P):
+                    cs = slice(c * P, (c + 1) * P)
+                    turned = psum.tile([P, PACK, P], F32, name="turned", tag="bank%d" % (6 + c))
+                    for t in range(PACK):
+                        nc.tensor.matmul(turned[:, t, :], gm[t // 2][:, t % 2, cs], ident[:], start=True, stop=False, is_transpose=True)
+                        nc.tensor.matmul(turned[:, t, :], gy[t // 2][:, t % 2, cs], ident[:], start=False, stop=True, is_transpose=True)
+                    zt = sb([P, S], BF16, "zt%d" % c, "zt_last" if c == BLK // P - 1 else None)
+                    nc.scalar.copy(zt[:].rearrange("j (u p e) -> j u p e", u=2, e=2), turned[:].rearrange("j (u e) p -> j u p e", e=2))
+                    for u in range(2):
+                        nc.tensor.transpose(back[:, c, u, :], zt[:].bitcast(F32)[:, u * P:(u + 1) * P], ident[:])
+                zb = sb([P, BLK * PACK], BF16, "zb0", "late_0")
+                nc.scalar.copy(zb[:].bitcast(F32).rearrange("p (c j u) -> p c j u", c=BLK // P, u=2), back[:].rearrange("p c u j -> p c j u"))
+            else:
+                z = sb([P, PACK, BLK], F32, "z%d" % b)
+                for t in range(PACK):
+                    nc.vector.scalar_tensor_tensor(z[:, t, :], y[t // 2][:, t % 2, :], gain[:, t:t + 1], gm[t // 2][:, t % 2, js], ALU.mult, ALU.add)
+                zb = sb([P, BLK * PACK], BF16, "zb1", "zt_last")
+                nc.scalar.copy(zb[:].rearrange("p (c i t) -> p c t i", i=4, t=PACK), z[:].rearrange("p t (c i) -> p c t i", i=4))
                 w2_words = code_words(k2_l, "w2w", "late_0")
-            nc.vector.quantize_mx(out=z_words[:, js].bitcast(FP8X4), scales=z_plane[:, js], in_=zb[:].rearrange("p j t -> p (j t)"))
+            nc.vector.quantize_mx(out=z_words[:, js].bitcast(FP8X4), scales=z_plane[:, js], in_=zb[:])
 
         out_t = out.rearrange("(p t) j -> t p j", t=PACK)
         neg = [sb([P, S], F32, "neg%d" % t) for t in range(PACK)]

@@ -113,20 +113,39 @@ def tile_picked_codetop2lap_none_p_kernel(tc, x_words, x_scales, d_words, d_scal
         def pair(name, width, tag=None):
             return [sb([P, 2, width], F32, "%s_%d" % (name, q), tag and "%s_%d" % (tag, q)) for q in range(2)]
 
-        a, du, mx, au, gm = (pair(name, S) for name in ("a", "du", "mx", "au", "gm"))
+        ident = sb([P, P], F32, "ident")
+        make_identity(nc, ident[:])
+        a, du, gm = (pair(name, S) for name in ("a", "du", "gm"))
+        mx = [sb([P, 2, S], F32, "mx_0")]
         for t in range(PACK):
             for js in halves:
                 nc.vector.tensor_copy(a[t // 2][:, t % 2, js], rowwin[t][:].indirect(entries(n1_l, js)))
             for js in halves:
                 nc.vector.tensor_tensor(du[t // 2][:, t % 2, js], rowwin[t][:].indirect(entries(n2_l, js)), a[t // 2][:, t % 2, js], ALU.subtract)
+            if t < 2:
+                up = sb([P, S], F32, "up%d" % t)
+                nc.scalar.activation(up[:], du[0][:, t, :], ACT.Relu)
+                turned = psum.tile([P, S], F32, name="mx_turned", tag="bank%d" % (4 + t))
+                back = psum.tile([P, S], F32, name="mx_back", tag="bank%d" % (6 + t))
+                for c in range(S // P):
+                    cs = slice(c * P, (c + 1) * P)
+                    nc.tensor.matmul(turned[:, cs], a[0][:, t, cs], ident[:], start=True, stop=False, is_transpose=True)
+                    nc.tensor.matmul(turned[:, cs], up[:, cs], ident[:], start=False, stop=True, is_transpose=True)
+                for b, js in enumerate(halves):
+                    mt = sb([P, BLK], F32, "mt%d_%d" % (t, b))
+                    nc.scalar.copy(mt[:], turned[:, js])
+                    for c in range(BLK // P):
+                        nc.tensor.transpose(back[:, js.start + c * P:js.start + (c + 1) * P], mt[:, c * P:(c + 1) * P], ident[:])
+                nc.scalar.copy(mx[0][:, t, :], back[:])
+        mx.append(sb([P, 2, S], F32, "mx_1", "mt1_0"))
+        for i in range(2):
+            nc.vector.scalar_tensor_tensor(mx[1][:, i, :], du[1][:, i, :], 0.0, a[1][:, i, :], ALU.max, ALU.add)
+        au = [sb([P, 2, S], F32, "au_%d" % q, "mt%d_1" % q) for q in range(2)]
         for q in range(2):
-            nc.vector.scalar_tensor_tensor(mx[q][:], du[q][:], 0.0, a[q][:], ALU.max, ALU.add)
             nc.scalar.activation(au[q][:], du[q][:], ACT.Abs, scale=0.5)
         for t in range(PACK):
             nc.scalar.activation(gm[t // 2][:, t % 2, :], mx[t // 2][:, t % 2, :], ACT.Copy, scale=half_gain[:, t:t + 1])
 
-        ident = sb([P, P], F32, "ident")
-        make_identity(nc, ident[:])
         z_words = sb([P, S], U32, "z_words")
         z_plane = sb([P, S], U8, "z_plane")
         w2_words = None

from contextlib import ExitStack

import concourse.mybir as mybir
from concourse.masks import make_identity

K, T, S, G, H = 512, 1024, 512, 2048, 512
FLOPS = 2 * 2 * K * H * S

F32 = mybir.dt.float32
BF16 = mybir.dt.bfloat16
I32 = mybir.dt.int32
U32 = mybir.dt.uint32
U16 = mybir.dt.uint16
U8 = mybir.dt.uint8
FP8X4 = mybir.dt.float8_e4m3fn_x4
ALU = mybir.AluOpType
ACT = mybir.ActivationFunctionType

P = 128
PACK = 4
BLK = 256
NBLK = S // BLK
LCOL = BLK // 16


def tile_picked_codetop2lap_none_p_kernel(tc, x_words, x_scales, d_words, d_scales, gs, offs, k1, n1, n2, n3, k2, n4, n5, out):
    nc = tc.nc
    with ExitStack() as ctx:
        keep = ctx.enter_context(tc.tile_pool(name="keep", bufs=1))
        psum = ctx.enter_context(tc.psum_pool(name="psum", bufs=1))

        def sb(shape, dtype, name, tag=None):
            return keep.tile(shape, dtype, name=name, tag=tag or name, align_bytes=64)

        def load_list(src, name):
            lst = sb([P, S // 16], U16, name)
            nc.sync.dma_start(lst[:], src)
            return lst

        d_bytes = sb([P, G], U8, "d_bytes")
        x_bytes = sb([P, T], U8, "x_bytes")
        nc.vector.memset(d_bytes[:].bitcast(I32), 0)
        nc.gpsimd.memset(x_bytes[:].bitcast(I32), 0)
        rowwin = [sb([P, S], F32, "rowwin%d" % t) for t in range(PACK)]
        halves = [slice(b * BLK, (b + 1) * BLK) for b in range(NBLK)]

        def entries(lst, js):
            return lst[:, js.start // 16:js.stop // 16]

        offs_l = load_list(offs, "offs_l")
        x_tab = sb([P, T], I32, "x_tab")
        nc.sync.dma_start(x_tab[:], x_words[0].rearrange("p n t -> p (n t)").bitcast(I32))
        k1_l = load_list(k1, "k1_l")
        d_rows = d_scales[0].bitcast(I32)
        for e in range(2):
            nc.sync.dma_start(d_bytes[:].bitcast(I32)[e:P:16, :], d_rows[e:16:2, :])
        x_rows = x_scales[0].bitcast(I32)
        for r in range(4):
            nc.sync.dma_start(x_bytes[:].bitcast(I32)[r:P:32, :], x_rows[r:16:4, :])
        d_tab = sb([P, G], I32, "d_tab")
        nc.sync.dma_start(d_tab[:], d_words[0].rearrange("p n t -> p (n t)").bitcast(I32))
        k2_l = load_list(k2, "k2_l")
        n1_l = load_list(n1, "n1_l")
        n2_l = load_list(n2, "n2_l")
        n3_l = load_list(n3, "n3_l")
        gain = sb([P, PACK], F32, "gain")
        nc.sync.dma_start(gain[:], gs.rearrange("(p t) o -> p (t o)", t=PACK))
        n4_l = load_list(n4, "n4_l")
        n5_l = load_list(n5, "n5_l")
        half_gain = sb([P, PACK], F32, "half_gain")
        nc.gpsimd.tensor_scalar_mul(half_gain[:], gain[:], 0.5)

        def pick(window, lst, dtype, name, tag=None):
            picked = sb([P, H], dtype, name, tag)
            for js in halves:
                nc.vector.tensor_copy(picked[:, js], window.indirect(entries(lst, js)))
            return picked

        def deal(picked, dtype, line, name):
            dealt = sb([P, H], dtype, name)
            for js in halves:
                ms = slice(js.start // PACK, js.stop // PACK)
                nc.vector.tensor_copy(dealt[:].rearrange("p (t m) -> p t m", t=PACK)[:, :, ms].rearrange("p t (c i) -> p c t i", i=line),
                                      picked[:, js].rearrange("p (c i t) -> p c t i", t=PACK, i=line))
            return dealt

        def code_plane(lst, name, tag=None):
            plane = deal(pick(d_bytes[:], lst, U8, name + "_picked", tag), U8, 16, name + "_plane")
            rows = plane[:].bitcast(I32)
            for e in range(2):
                nc.scalar.dma_start(rows[2 + e:P:32, :], rows[16 + e:P:32, :])
            return plane

        def code_words(lst, name, tag=None):
            return deal(pick(d_tab[:].bitcast(U32), lst, U32, name + "_picked", tag), U32, 4, name + "_dealt")

        x_sel = sb([P, S], U32, "x_sel")
        nc.vector.tensor_copy(x_sel[:], x_tab[:].bitcast(U32).indirect(offs_l[:]))
        w1_plane = code_plane(k1_l, "w1s")
        x_plane = sb([P, S], U8, "x_plane")
        nc.vector.tensor_copy(x_plane[:], x_bytes[:].indirect(offs_l[:]))
        w1_words = code_words(k1_l, "w1w")

        for t in range(PACK):
            cols = slice(t * P, (t + 1) * P)
            acc = psum.tile([P, S], F32, name="acc1", tag="bank%d" % t)
            nc.tensor.matmul_mx(out=acc[:], lhsT=w1_words[:, cols].bitcast(FP8X4), lhsT_scale=w1_plane[:, cols],
                                rhs=x_sel[:].bitcast(FP8X4), rhs_scale=x_plane[:], start=True, stop=True)
            nc.scalar.activation(rowwin[t][:], acc[:], ACT.Copy, scale=0.0625)

        w2_plane = code_plane(k2_l, "w2s", "w1w_picked")

        def pair(name, width, tag=None):
            return [sb([P, 2, width], F32, "%s_%d" % (name, q), tag and "%s_%d" % (tag, q)) for q in range(2)]

        ident = sb([P, P], F32, "ident")
        make_identity(nc, ident[:])
        a, du, gm = (pair(name, S) for name in ("a", "du", "gm"))
        mx = [sb([P, 2, S], F32, "mx_0")]
        for t in range(PACK):
            for js in halves:
                nc.vector.tensor_copy(a[t // 2][:, t % 2, js], rowwin[t][:].indirect(entries(n1_l, js)))
            for js in halves:
                nc.vector.tensor_tensor(du[t // 2][:, t % 2, js], rowwin[t][:].indirect(entries(n2_l, js)), a[t // 2][:, t % 2, js], ALU.subtract)
            if t < 2:
                up = sb([P, S], F32, "up%d" % t)
                nc.scalar.activation(up[:], du[0][:, t, :], ACT.Relu)
                turned = psum.tile([P, S], F32, name="mx_turned", tag="bank%d" % (4 + t))
                back = psum.tile([P, S], F32, name="mx_back", tag="bank%d" % (6 + t))
                for c in range(S // P):
                    cs = slice(c * P, (c + 1) * P)
                    nc.tensor.matmul(turned[:, cs], a[0][:, t, cs], ident[:], start=True, stop=False, is_transpose=True)
                    nc.tensor.matmul(turned[:, cs], up[:, cs], ident[:], start=False, stop=True, is_transpose=True)
                for b, js in enumerate(halves):
                    mt = sb([P, BLK], F32, "mt%d_%d" % (t, b))
                    nc.scalar.copy(mt[:], turned[:, js])
                    for c in range(BLK // P):
                        nc.tensor.transpose(back[:, js.start + c * P:js.start + (c + 1) * P], mt[:, c * P:(c + 1) * P], ident[:])
                nc.scalar.copy(mx[0][:, t, :], back[:])
        mx.append(sb([P, 2, S], F32, "mx_1", "mt1_0"))
        for i in range(2):
            nc.vector.scalar_tensor_tensor(mx[1][:, i, :], du[1][:, i, :], 0.0, a[1][:, i, :], ALU.max, ALU.add)
        au = [sb([P, 2, S], F32, "au_%d" % q, "mt%d_1" % q) for q in range(2)]
        for q in range(2):
            nc.scalar.activation(au[q][:], du[q][:], ACT.Abs, scale=0.5)
        for t in range(PACK):
            nc.scalar.activation(gm[t // 2][:, t % 2, :], mx[t // 2][:, t % 2, :], ACT.Copy, scale=half_gain[:, t:t + 1])

        z_words = sb([P, S], U32, "z_words")
        z_plane = sb([P, S], U8, "z_plane")
        w2_words = None
        for b in range(NBLK):
            js = slice(b * BLK, (b + 1) * BLK)
            v = pair("v%d" % b, BLK, "v")
            for t in range(PACK):
                nc.vector.tensor_tensor(v[t // 2][:, t % 2, :], rowwin[t][:].indirect(n3_l[:, b * LCOL:(b + 1) * LCOL]),
                                        mx[t // 2][:, t % 2, js], ALU.subtract)
            low = pair("low%d" % b, BLK)
            y = pair("y%d" % b, BLK)
            for q in range(2):
                nc.vector.scalar_tensor_tensor(low[q][:], v[q][:], -0.5, au[q][:, :, js], ALU.mult, ALU.min)
            for q in range(2):
                nc.vector.tensor_tensor(y[q][:], v[q][:], low[q][:], ALU.max)
            if b == 0:
                gy = pair("gy", BLK)
                for t in range(PACK):
                    nc.scalar.activation(gy[t // 2][:, t % 2, :], y[t // 2][:, t % 2, :], ACT.Copy, scale=gain[:, t:t + 1])
                back = psum.tile([P, BLK // P, 2, P], F32, name="back", tag="bank0")
                for c in range(BLK // P):
                    cs = slice(c * P, (c + 1) * P)
                    turned = psum.tile([P, PACK, P], F32, name="turned", tag="bank%d" % (6 + c))
                    for t in range(PACK):
                        nc.tensor.matmul(turned[:, t, :], gm[t // 2][:, t % 2, cs], ident[:], start=True, stop=False, is_transpose=True)
                        nc.tensor.matmul(turned[:, t, :], gy[t // 2][:, t % 2, cs], ident[:], start=False, stop=True, is_transpose=True)
                    zt = sb([P, S], BF16, "zt%d" % c, "zt_last" if c == BLK // P - 1 else None)
                    nc.scalar.copy(zt[:].rearrange("j (u p e) -> j u p e", u=2, e=2), turned[:].rearrange("j (u e) p -> j u p e", e=2))
                    for u in range(2):
                        nc.tensor.transpose(back[:, c, u, :], zt[:].bitcast(F32)[:, u * P:(u + 1) * P], ident[:])
                zb = sb([P, BLK * PACK], BF16, "zb0", "late_0")
                nc.scalar.copy(zb[:].bitcast(F32).rearrange("p (c j u) -> p c j u", c=BLK // P, u=2), back[:].rearrange("p c u j -> p c j u"))
            else:
                z = sb([P, PACK, BLK], F32, "z%d" % b)
                for t in range(PACK):
                    nc.vector.scalar_tensor_tensor(z[:, t, :], y[t // 2][:, t % 2, :], gain[:, t:t + 1], gm[t // 2][:, t % 2, js], ALU.mult, ALU.add)
                zb = sb([P, BLK * PACK], BF16, "zb1", "zt_last")
                nc.scalar.copy(zb[:].rearrange("p (c i t) -> p c t i", i=4, t=PACK), z[:].rearrange("p t (c i) -> p c t i", i=4))
                w2_words = code_words(k2_l, "w2w", "late_0")
            nc.vector.quantize_mx(out=z_words[:, js].bitcast(FP8X4), scales=z_plane[:, js], in_=zb[:])

        out_t = out.rearrange("(p t) j -> t p j", t=PACK)
        neg = [sb([P, S], F32, "neg%d" % t) for t in range(PACK)]
        part = [sb([P, S], F32, "part%d" % t) for t in range(PACK)]
        res = [sb([P, S], F32, "res%d" % t) for t in range(PACK)]

        def product2(t, js, bank):
            cols = slice(t * P, (t + 1) * P)
            acc = psum.tile([P, js.stop - js.start], F32, name="acc2", tag="bank%d" % bank)
            nc.tensor.matmul_mx(out=acc[:], lhsT=w2_words[:, cols].bitcast(FP8X4), lhsT_scale=w2_plane[:, cols],
                                rhs=z_words[:, js].bitcast(FP8X4), rhs_scale=z_plane[:, js], start=True, stop=True)
            return acc

        def first(t, js):
            nc.vector.tensor_tensor(part[t][:, js], rowwin[t][:].indirect(n4_l[:, js.start // 16:js.stop // 16]), neg[t][:, js], ALU.add)

        def second(t, js):
            nc.vector.tensor_tensor(res[t][:, js], rowwin[t][:].indirect(n5_l[:, js.start // 16:js.stop // 16]), part[t][:, js], ALU.add)
            nc.sync.dma_start(out_t[t][:, js], res[t][:, js])

        whole = slice(0, S)
        acc0 = [product2(0, js, 4 + b) for b, js in enumerate(halves)]
        for b, js in enumerate(halves):
            nc.scalar.activation(rowwin[0][:, js], acc0[b][:], ACT.Copy, scale=0.75 * 0.0625)
        nc.vector.tensor_scalar_mul(neg[0][:, halves[0]], acc0[0][:], -0.0625)
        nc.scalar.activation(neg[0][:, halves[1]], acc0[1][:], ACT.Copy, scale=-0.0625)
        for t in range(1, PACK):
            acc = product2(t, whole, t)
            nc.scalar.activation(rowwin[t][:, whole], acc[:], ACT.Copy, scale=0.75 * 0.0625)
            nc.scalar.activation(neg[t][:], acc[:], ACT.Copy, scale=-0.0625)
        for t in range(PACK):
            for js in halves:
                first(t, js)
            for js in halves:
                second(t, js)
